import numpy as np, ml_dtypes
CORES = [16,18,20,22]
N = 4
BF = ml_dtypes.bfloat16
W, V, Q, S, RO = 4096, 256, 2, 1, 4
RK = np.arange(N)[:, None, None]; GR = np.arange(8)[None, :, None]; VE = np.arange(V)[None, None, :]
def unfold(a, m):
    return np.ascontiguousarray(a.reshape(N, 8, 16, m).transpose(0, 1, 3, 2))
def fold(a):
    return np.ascontiguousarray(a.transpose(0, 1, 3, 2)).reshape(N, 128, -1)
def pack(T, U, P, x):
    return {"tx": fold(T).astype(np.float32).astype(BF), "pu": fold(U).astype(np.int32), "p0": fold(P).astype(np.int32), "x0": fold(x).astype(np.float32).astype(BF)}
def pair(rng, P):
    m = rng.integers(0, 17, (N, 8, V // 2, 1))
    P[:, :, 1::2] = np.where(np.arange(16) < m, P[:, :, 0::2], P[:, :, 1::2])
    return P
def parts(rng):
    T = rng.integers(0, 128, (N, 8, W, 16)); U = rng.integers(0, W, (N, 8, W, 16))
    U = np.where(rng.random((N, 8, W, 1)) < 0.25, U[..., :1], U)
    P = rng.integers(0, W, (N, 8, V, 16))
    for k in range(1, 16):
        nxt = U[RK, GR, P[..., k - 1], rng.integers(0, 16, (N, 8, V))]
        P[..., k] = np.where(rng.random((N, 8, V)) < 0.5, nxt, P[..., k])
    P = pair(rng, P)
    near = np.clip(T[RK, GR, P[..., 15]] + rng.integers(-20, 21, (N, 8, V, 16)), 0, 127)
    x = np.where(rng.random((N, 8, V, 1)) < 0.5, near, rng.integers(0, 128, (N, 8, V, 16)))
    return T, U, P, x
def setup_inputs(rng):
    return pack(*parts(rng))
def setup_inputs_ties(rng):
    T, U, P, x = parts(rng)
    few = rng.integers(0, 128, (N, 8, 6, 16)); few[:, :, 0] = 0; few[:, :, 1] = 127
    T = few[RK, GR, rng.integers(0, 6, (N, 8, W))]; x = few[RK, GR, rng.integers(0, 6, (N, 8, V))]
    return pack(T, U, P, x)
def setup_inputs_cuts(rng):
    T, U, P, x = parts(rng); h = W // 2; s = V // 4
    for g in range(8):
        o = rng.permutation(W); P[:, g] = o[h + P[:, g] % h]
        for j in range(s):
            m = (1, Q - 1, Q, N)[j if j < 4 else int(rng.integers(0, 4))]
            nm = o[s + np.arange(N)]; nm[rng.permutation(N)[:m]] = o[j]
            P[:, g, 2 * j + 1] = P[:, g, 2 * j]; P[:, g, 2 * j:2 * j + 2, 15] = nm[:, None]
    return pack(T, U, P, x)
def setup_inputs_crowd(rng):
    T, U, P, x = parts(rng); h = V // 2; r = np.arange(N)[:, None]; j = np.arange(h)[None, :]
    for g in (0, 1, 2, 3, 4, 5, 7):
        o = rng.permutation(W); nm = np.repeat(o[1:N + 1, None], V, axis=1); n = N + 1
        if g in (0, 7):
            if g == 7: o = np.concatenate([np.array([W - 1]), rng.permutation(W - 1)])
            nm = np.stack([rng.permutation(o[i * V:(i + 1) * V]) for i in np.minimum(rng.permutation(N) // Q, N // Q - 1)]); n = (N // Q) * V
        elif g in (1, 4):
            o = 1 + rng.permutation(W - 1); n = ((N - 1) // (Q - 1) + 1) * h
            nm = o[(rng.permutation(N) // (Q - 1))[:, None] * h + np.arange(V)[None, :] // 2]
        elif g == 2: nm[rng.permutation(N)[:Q]] = o[0]
        elif g == 5:
            s = int(rng.integers(0, N - Q + 1)); nm[s:s + Q - 1, :192] = o[0]; nm = nm[:, rng.permutation(V)]
        else: o = np.arange(W)[::-1]; n = 512
        a, b = o[:n], o[n:]
        T[:, g] = T[:, g] >> 2; x[:, g] = x[:, g] >> 2; T[:, g, a] = T[:, g, a] + 96
        P[:, g] = b[P[:, g] % len(b)]; U[:, g] = b[U[:, g] % len(b)]; P[:, g, 1::2] = np.array(P[:, g, 0::2])
        if g == 3:
            m = rng.integers(1, 15, (N, h)); c = W - 512 + 4 * rng.integers(0, 128, (N, h))
            P[r, g, 2 * j, m] = c; P[r, g, 2 * j + 1, m] = c + 1
        else: P[:, g, :, 15] = nm
        if g in (0, 7): P[:, g, :, 14] = np.array(P[:1, g, :, 14]); U[:, g] = np.array(U[:1, g, :, :1])
    return pack(T, U, P, x)
def setup_inputs_few(rng):
    T, U, P, x = parts(rng)
    for g in (0, 2, 4, 6):
        a = np.concatenate([np.array([0, W - 1]), rng.integers(0, W, 10)]); P[:, g] = a[P[:, g] % 12]
        if g in (0, 4): U[:, g] = a[U[:, g] % 12]
    P[:, 2] = np.array(P[:, 2, :, :1]); U[:, 4, ::2] = rng.integers(0, W, (N, W // 2, 16)); U[:, 6] = np.arange(W)[:, None]
    return pack(T, U, P, x)
def setup_inputs_spread(rng):
    T = np.minimum((np.exp2(7 * rng.random((N, 8, W, 1))) * rng.random((N, 8, W, 16))).astype(np.int64), 127)
    x = np.minimum((np.exp2(7 * rng.random((N, 8, V, 1))) * rng.random((N, 8, V, 16))).astype(np.int64), 127)
    U = np.minimum((W * rng.random((N, 8, W, 16)) ** 2).astype(np.int64), W - 1)
    P = np.minimum((W * rng.random((N, 8, V, 16)) ** 3).astype(np.int64), W - 1)
    return pack(T, U, pair(rng, P), x)
def check_inputs(d):
    bad = []
    for k, hi in (("tx", 127), ("pu", W - 1), ("p0", W - 1), ("x0", 127)):
        a = np.asarray(d[k]).astype(np.float64)
        if not (np.all(a >= 0) and np.all(a <= hi)): bad.append("range of " + k)
        elif np.any(np.floor(a) != a): bad.append("whole numbers of " + k)
    return bad
def reference(tx, pu, p0, x0):
    T = unfold(tx.astype(np.float32).astype(np.int32), W); U = unfold(pu.astype(np.int64), W)
    P = unfold(p0.astype(np.int64), V); x = unfold(x0.astype(np.float32).astype(np.int32), V)
    row = np.arange(16); cut = np.zeros((8, W), bool); R4 = RK[..., None]; G4 = GR[..., None]
    for rnd in range(RO):
        d = np.add.reduce(np.abs(T[R4, G4, P] - x[:, :, :, None, :]), axis=4)
        differ = P != P[:, :, np.arange(V) ^ 1]
        q = np.where(np.any(differ, axis=3), np.argmax(differ, axis=3), 15)
        f = np.argmax(np.where(row >= np.maximum(q, 1)[..., None], d, -1), axis=3)
        old = cut[G4, P] & (row >= 1)
        k = np.where(np.any(old, axis=3), np.argmax(old, axis=3), f)
        charged = np.zeros((N, 8, W), bool); charged[RK, GR, P[RK, GR, VE, f]] = True
        cut = cut | (np.add.reduce(charged.astype(np.int64), axis=0) >= Q)
        T[:, cut] = 256
        pup = U[RK, GR, P[RK, GR, VE, k - 1]]
        e = np.add.reduce(np.abs(T[R4, G4, pup] - x[:, :, :, None, :]), axis=4)
        b = np.argmin(e, axis=3); best = pup[RK, GR, VE, b]
        take = e[RK, GR, VE, b] < d[RK, GR, VE, k]
        P[RK, GR, VE, k] = np.where(take, best, P[RK, GR, VE, k])
        x = np.where(take[..., None], (x + T[RK, GR, best]) >> 1, x)
        if rnd + 1 < RO: P = np.roll(P, S, axis=0); x = np.roll(x, S, axis=0)
    return {"yp": fold(P).astype(np.float32), "yx": fold(x).astype(np.float32).astype(BF), "yc": np.repeat(cut[None], N, axis=0).astype(np.float32)}

@@ -1,0 +1,400 @@
+from concourse.bass import DstId, RemoteDMATransfer
+from concourse.mybir import AluOpType, ActivationFunctionType
+
+R = 4
+BIG = 16384.0
+TOP = 8388608
+
+SCRATCH = {}
+SHAPES = {
+    "bfloat16": "TX 4096 X0 256 D 4112 AB 4096 OA 2048 OX 1024 OB 4096 LS 2048 IDM 128 IDN 128 IDB 128 IDT 128 GR 768 IOM 128 IM 128 IOB 256 "
+                "CKC 256 CKE 256 NEG 256 ONE 8 NE 128 TA 256 TCH 256 FB 32 XN 256 YX 256",
+    "int32": "PUW 4096 P0 256 I1 16 I2 16 I3 16 I5 16 PERMI 16 REPI 16 VS 16 GI 16 HI 16 FI 32 FM 32 KS 16 TH 16 EI 32 EM 32 ET 16 LT 16 "
+             "JJ 16 PO 16",
+    "uint16": "PERM 16 PERM2 32 REP 16 TL 32 CU 256 POU 16",
+    "float32": "MKI 512 MK 512 CL 256 COLS 16 COLP 16 COLH 16 SW 512 SWT 512 AA 256 BB 256 RA 256 RB 256 SK 256 KT 256 OH 256 PR 256 TF 16 "
+               "CF 256 CB 256 QR 256 OLD 16 X2 256 N1 16 BN 16 DL 16 DT 16 UP 256 YP 256 YC 256",
+}
+for _d, _l in SHAPES.items():
+    _w = _l.split()
+    for _n, _c in zip(_w[::2], _w[1::2]):
+        SCRATCH[_n] = ("sbuf", [128, int(_c)], _d)
+for _n in ("pcr", "pcnt", "pchg", "pcut", "pd0", "pd1", "pd2", "pd3"):
+    SCRATCH[_n] = ("psum", [128, 512], "float32")
+for _r in range(R):
+    SCRATCH["XR%d" % _r] = ("sbuf", [128, 1024], "bfloat16")
+    SCRATCH["PU%d" % _r] = ("sbuf", [128, 256], "uint16")
+    SCRATCH["M%d" % _r] = ("sbuf", [128, 768], "float32")
+    SCRATCH["XS%d" % _r] = ("sbuf", [128, 256], "bfloat16")
+    SCRATCH["PS%d" % _r] = ("sbuf", [128, 256], "uint16")
+    SCRATCH["MS%d" % _r] = ("sbuf", [128, 768], "float32")
+    SCRATCH["FS%d" % _r] = ("sbuf", [128, 256], "bfloat16")
+    SCRATCH["FR%d" % _r] = ("sbuf", [128, 768], "bfloat16")
+for _r in range(R + 1):
+    SCRATCH["T0%d" % _r] = ("sbuf", [128, 256], "bfloat16")
+
+SEMAPHORES = ["qv", "qs", "qt", "qg", "ls", "dx0", "dp0", "dtx", "dpu", "dt0", "dyp", "dyx", "dyc"]
+SEMAPHORES += ["%s%d" % (a, r) for a in ("a1", "a2", "fl", "dc") for r in range(R)]
+
+
+def rank_program(g, core, T, topo):
+    rank = T.rank_of(core)
+    if rank is None:
+        return
+    OP = AluOpType
+    AF = ActivationFunctionType
+    eng = {"v": g.vector, "s": g.scalar, "t": g.tensor, "g": g, "y": g.sync}
+    cnt = {"v": 0, "s": 0, "t": 0, "g": 0}
+    known = {e: {} for e in eng}
+    acc = {}
+
+    def B(name, lo=0, hi=None, step=1):
+        if hi is None:
+            hi = SCRATCH[name][1][1]
+        ap = T[name][:, lo:hi] if step == 1 else T[name][:, lo:hi:step]
+        return (name, lo, hi, ap)
+
+    def psum(name):
+        return SCRATCH[name][0] == "psum"
+
+    def need(e, reads, writes):
+        deps = {}
+        for w, specs in ((False, reads), (True, writes)):
+            for name, lo, hi, _ in specs:
+                for plo, phi, pw, pe, tok in acc.get(name, ()):
+                    if pe == e:
+                        hit = e != "t" and pw and not w and lo < phi and plo < hi
+                    elif psum(name):
+                        hit = True
+                    else:
+                        hit = (pw or w) and lo < phi and plo < hi
+                    if hit and deps.get(tok[0], 0) < tok[1]:
+                        deps[tok[0]] = tok[1]
+        for sem in sorted(deps):
+            if known[e].get(sem, 0) < deps[sem]:
+                eng[e].wait_ge(T.sem[sem], deps[sem])
+                known[e][sem] = deps[sem]
+
+    def mark(pe, tok, reads, writes):
+        for name, lo, hi, _ in writes:
+            old = [a for a in acc.get(name, ()) if not (lo <= a[0] and a[1] <= hi)]
+            acc[name] = old + [(lo, hi, True, pe, tok)]
+        for name, lo, hi, _ in reads:
+            old = [a for a in acc.get(name, ()) if not (a[3] == pe and not a[2] and lo <= a[0] and a[1] <= hi)]
+            acc[name] = old + [(lo, hi, False, pe, tok)]
+
+    def op(e, reads, writes, fn):
+        need(e, reads, writes)
+        fn().then_inc(T.sem["q" + e], 1)
+        cnt[e] += 1
+        mark(e, ("q" + e, cnt[e]), reads, writes)
+
+    def dma(e, sem, out, in_, reads, writes):
+        need(e, reads, writes)
+        eng[e].dma_start(out, in_).then_inc(T.sem[sem], 16)
+        mark("d" + sem, (sem, 16), reads, writes)
+
+    def tt(out, a, b, o):
+        op("v", [a, b], [out], lambda: g.vector.tensor_tensor(out[3], a[3], b[3], o))
+
+    def ts(out, a, s1, o1, s2=None, o2=None):
+        reads = [a] + [s for s in (s1,) if isinstance(s, tuple)]
+        x = s1[3] if isinstance(s1, tuple) else s1
+        if o2 is None:
+            op("v", reads, [out], lambda: g.vector.tensor_scalar(out[3], a[3], x, None, o1))
+        else:
+            op("v", reads, [out], lambda: g.vector.tensor_scalar(out[3], a[3], x, s2, o1, o2))
+
+    def cp(out, a):
+        op("v", [a], [out], lambda: g.vector.tensor_copy(out[3], a[3]))
+
+    def gat(out, win, lst, b, o):
+        if b is None:
+            op("v", [win, lst], [out], lambda: g.vector.tensor_copy(out[3], win[3].indirect(lst[3])))
+        else:
+            op("v", [win, lst, b], [out], lambda: g.vector.tensor_tensor(out[3], win[3].indirect(lst[3]), b[3], o))
+
+    def fill(out, value):
+        op("v", [], [out], lambda: g.vector.memset(out[3], value))
+
+    def act(out, a, f, scale=1.0, bias=0.0):
+        col = isinstance(bias, tuple)
+        x = bias[3] if col else bias
+        op("s", [a, bias] if col else [a], [out], lambda: g.scalar.activation(out[3], a[3], f, bias=x, scale=scale))
+
+    def mm(out, lhsT, rhs, start, stop):
+        op("t", [lhsT, rhs], [out], lambda: g.tensor.matmul(out[3], lhsT[3], rhs[3], start, stop))
+
+    def iota(name, pattern, base, cm):
+        out = B(name)
+        if SCRATCH[name][2] == "int32":
+            op("g", [], [out], lambda: g.iota(out[3], pattern, base, cm))
+        else:
+            op("g", [], [out], lambda: g.iota(out[3], pattern, base, cm, allow_small_or_imprecise_dtypes=True))
+
+    def tree(out, src, o):
+        tt(B("KT", 0, 128), B(src, 0, 128), B(src, 128, 256), o)
+        tt(B("KT", 128, 192), B("KT", 0, 64), B("KT", 64, 128), o)
+        tt(B("KT", 192, 224), B("KT", 128, 160), B("KT", 160, 192), o)
+        tt(out, B("KT", 192, 208), B("KT", 208, 224), o)
+
+    def swap_in(win, lst):
+        gat(B("SW"), win, lst, B("MK"), OP.mult)
+        op("v", [B("SW")], [B("SWT")], lambda: g.vector.transpose(T.SWT[:, :], T.SW[:, :]))
+
+    def swap_out(name):
+        for t in range(16):
+            tt(B(name, 16 * t, 16 * t + 16), B("SWT", t, 512, 32), B("SWT", 16 + t, 512, 32), OP.add)
+
+    def high(src, ta):
+        act(ta, src, AF.Identity, scale=1.0 / 256.0, bias=159.502)
+
+    def minus257(ta):
+        act(B("pcr", 256, 512), ta, AF.Identity, scale=-257.0, bias=257.0 * 160.0)
+
+    def prep(m):
+        tt(B("NE"), B(m, 0, 256, 2), B(m, 1, 256, 2), OP.not_equal)
+        high(B(m, 0, 256), B("TA"))
+        minus257(B("TA"))
+        for k in range(16):
+            mm(B("pcnt", 8 * k, 128), B("IDT"), B("NE", 0, 128 - 8 * k), k == 0, False)
+        mm(B("pcnt", 120, 128), B("IDT"), B("ONE"), False, True)
+        tt(B(m, 512, 768), B(m, 0, 256), B("pcr", 256, 512), OP.add)
+        for p in (0, 1):
+            tt(B(m, 256 + p, 512, 2), B("pcnt", 0, 128), B("CL", p, 256, 2), OP.min)
+
+    def distances(lst, xr, ck, ta, raw, chunks, later, keep):
+        op("s", [B("TX"), B(lst, 16 * raw, 16 * raw + 48)], [B("GR")],
+           lambda: g.scalar.activation(T.GR[:, :], T.TX[:, :].indirect(B(lst, 16 * raw, 16 * raw + 48)[3]), AF.Copy))
+        two, one = B("pcnt", 0, 512), B("pchg", 0, 256)
+        mm(two, B("IDM"), B("GR", 0, 512), True, False)
+        mm(two, B("IDN"), B(xr, 0, 512), False, True)
+        mm(one, B("IDM"), B("GR", 512, 768), True, False)
+        mm(one, B("IDN"), B(xr, 0, 256), False, True)
+        wait = []
+        for q, calls in enumerate(chunks):
+            for ka, kb in calls:
+                gat(B("D", 16 + 256 * ka, 16 + 256 * kb), B("TX"), B(lst, 16 * ka, 16 * kb), B(xr, 0, 256 * (kb - ka)), OP.subtract)
+            for ka, kb in ([(calls[0][0], calls[-1][1])] if q < 3 else calls):
+                act(B("AB", 256 * ka, 256 * kb), B("D", 16 + 256 * ka, 16 + 256 * kb), AF.Abs)
+            ka, kb = calls[0][0], calls[-1][1]
+            if q == 0:
+                act(B("AB", 256 * raw, 256 * raw + 512), two, AF.Abs)
+                act(B("AB", 256 * raw + 512, 256 * raw + 768), one, AF.Abs)
+                ka = raw
+            if q == 1:
+                later()
+            ps = B("pd%d" % q, 0, 16 * (kb - ka))
+            mm(ps, B("IDM"), B(ck, 16 * ka, 16 * kb), True, False)
+            for s in range(16):
+                mm(ps, B("LS", 128 * s, 128 * s + 128), B("AB", 256 * ka + s, 256 * kb, 16), False, False)
+            wait.append((ps, B(ta, 16 * ka, 16 * kb)))
+            while q > 0 and wait:
+                ps, dig = wait.pop(0)
+                mm(ps, B("IDM"), dig, False, True)
+        if keep:
+            act(B("D", 16 + 256 * raw, 16 + 256 * raw + 512), two, AF.Copy)
+            act(B("D", 16 + 256 * raw + 512, 16 + 256 * raw + 768), one, AF.Copy)
+
+    dma("y", "dp0", T.P0[:, :], T.p0[:, :], [], [B("P0")])
+    dma("y", "dx0", T.X0[:, :], T.x0[:, :], [], [B("X0")])
+    dma("y", "dtx", T.TX[:, :], T.tx[:, :], [], [B("TX")])
+    dma("y", "dt0", T.T00[:, :], T.tx[0:128:16, :], [], [B("T00")])
+    g.sync.wait_ge(T.sem.dtx, 16)
+    dma("y", "dpu", T.PUW[:, :], T.pu[:, :], [], [B("PUW")])
+
+    iota("I1", [[1, 16]], 0, 16)
+    iota("I2", [[0, 16]], 0, 1)
+    iota("MKI", [[0, 16], [1, 2], [0, 16]], 0, 0)
+    iota("IOM", [[1, 128]], 0, 0)
+    iota("I5", [[1, 16]], 0, 0)
+    iota("I3", [[16, 16]], 16, 0)
+    iota("CL", [[-256, 16], [0, 16]], TOP + 4096 + 255, 0)
+    iota("CKC", [[-256, 16], [0, 16]], 4096 - 160, 0)
+    iota("IOB", [[1, 256]], 0, 0)
+    iota("CKE", [[256, 16], [0, 16]], -160, 0)
+    fill(B("ONE"), 1.0)
+    fill(B("NEG"), -1.0)
+    fill(B("D", 0, 16), 0.0)
+    fill(B("AA", 0, 16), 0.0)
+    fill(B("PR", 0, 16), 0.0)
+    fill(B("SK", 0, 16), 0.0)
+    ts(B("PERMI"), B("I1"), 255, OP.bitwise_and)
+    ts(B("HI"), B("I2"), 16, OP.bitwise_and, 4, OP.logical_shift_right)
+    ts(B("REPI"), B("I2"), 15, OP.bitwise_and)
+    ts(B("GI"), B("I2"), 112, OP.bitwise_and)
+    cp(B("PERM"), B("PERMI"))
+    cp(B("PERM2", 0, 32, 2), B("PERMI"))
+    cp(B("PERM2", 1, 32, 2), B("PERMI"))
+    cp(B("COLH"), B("HI"))
+    cp(B("COLP"), B("I2"))
+    cp(B("REP"), B("REPI"))
+    ts(B("MK"), B("MKI"), B("COLH", 0, 1), OP.is_equal)
+    tt(B("COLS"), B("GI"), B("I5"), OP.add)
+    tt(B("VS"), B("REPI"), B("I3"), OP.add)
+    ts(B("IDM"), B("IOM"), B("COLP", 0, 1), OP.is_equal)
+    ts(B("IDN"), B("IOM"), B("COLP", 0, 1), OP.is_equal, -1.0, OP.mult)
+    swap_in(B("P0"), B("PERM2"))
+    swap_out("M0")
+    cp(B("PU0"), B("M0", 0, 256))
+    gat(B("XR0", 0, 256), B("X0"), B("PERM"), None, None)
+    ts(B("IDT"), B("IOM"), B("COLP", 0, 1), OP.is_equal, 16777216.0, OP.mult)
+    ts(B("IDB"), B("IOM"), B("COLP", 0, 1), OP.is_equal, BIG, OP.mult)
+    ts(B("IM"), B("IOM"), B("COLS", 0, 1), OP.subtract)
+    fill(B("CL", 0, 16), 0.0)
+    for s in range(16):
+        ts(B("LS", 128 * s, 128 * s + 128), B("IOM"), B("COLS", s, s + 1), OP.is_equal, 4096.0, OP.mult)
+    prep("M0")
+
+    others = [q for q in range(R) if q != rank]
+    nxt, prv = T.cores[(rank + 1) % R], T.cores[(rank - 1) % R]
+    sent = 0
+    for r in range(R):
+        xr, pu, m, last = "XR%d" % r, "PU%d" % r, "M%d" % r, r == R - 1
+
+        def chain_arrays():
+            if r > 0:
+                high(B(m, 0, 256), B("TA"))
+            act(B("pcr", 0, 256), B(m, 0, 256), AF.Copy)
+
+        act(B(xr, 256, 512), B(xr, 0, 256), AF.Copy)
+        distances(pu, xr, "CKC", "TA", 1, [[(4, 5)], [(5, 7), (7, 9)], [(9, 11), (11, 13)], [(13, 15), (15, 16)]], chain_arrays, False)
+        act(B(xr, 512, 1024), B(xr, 0, 512), AF.Copy)
+        rows = [(1, 5), (5, 9), (9, 13), (13, 16)]
+        for q, (ka, kb) in enumerate(rows):
+            ka, kb = 16 * ka, 16 * kb
+            tt(B("AA", ka, kb), B("pd%d" % q, 0, kb - ka), B(m, 256 + ka, 256 + kb), OP.min)
+            tt(B("BB", ka, kb), B("AA", ka, kb), B(m, 512 + ka, 512 + kb), OP.add)
+            for src, run in (("AA", "RA"), ("BB", "RB")):
+                if q == 1:
+                    tt(B(run, 0, 64), B(src, 16, 80), B(src, 80, 144), OP.max)
+                elif q == 2:
+                    tt(B(run, 64, 128), B(run, 0, 64), B(src, 144, 208), OP.max)
+                elif q == 3:
+                    tt(B(run, 64, 112), B(run, 64, 112), B(src, 208, 256), OP.max)
+        for run in ("RA", "RB"):
+            tt(B(run, 128, 160), B(run, 64, 96), B(run, 96, 128), OP.max)
+        for j, run in enumerate(("RA", "RB")):
+            tt(B("FI", 16 * j, 16 * j + 16), B(run, 128, 144), B(run, 144, 160), OP.max)
+        ts(B("FM"), B("FI"), 255, OP.bitwise_and)
+        cp(B("FB"), B("FM"))
+        for c in range(16):
+            if c < 8:
+                ts(B("OA", 128 * c, 128 * c + 128), B("IM"), B("FB", c, c + 1), OP.is_equal)
+            else:
+                j = c - 8
+                act(B("OX", 128 * j, 128 * j + 128), B("IM"), AF.Abs, scale=-1.0, bias=B("FB", c, c + 1))
+                if c % 4 == 3:
+                    act(B("OA", 128 * c - 384, 128 * c + 128), B("OX", 128 * j - 384, 128 * j + 128), AF.Relu, scale=-1.0, bias=1.0)
+            ts(B("OB", 256 * c, 256 * c + 256), B("IOB"), B("FB", 16 + c, 17 + c), OP.is_equal)
+        for c in range(16):
+            mm(B("pchg", 0, 256), B("OA", 128 * c, 128 * c + 128), B("OB", 256 * c, 256 * c + 256), c == 0, c == 15)
+        mm(B("pcut", 0, 256), B("IDM"), B("T0%d" % r), True, False)
+        mm(B("pcut", 0, 256), B("IDB"), B("NEG"), False, False)
+        if r > 0:
+            for q, (ka, kb) in enumerate(rows):
+                act(B("pcnt", 16 * ka, 16 * kb), B("pd%d" % q, 0, 16 * (kb - ka)), AF.Relu, bias=-16777216.0)
+        act(B("FS%d" % r), B("pchg", 0, 256), AF.Sign)
+        mm(B("pcut", 0, 256), B("IDB"), B("FS%d" % r), False, False)
+        need("g", [B("FS%d" % r)], [])
+        dsts, ids = [], []
+        for q in others:
+            j = (rank - q - 1) % R
+            rid, pid = topo.addr(T.cores[q])[:2]
+            ids.append(DstId(rid=rid, pnc=pid))
+            dsts.append(T["FR%d" % r][:, 256 * j:256 * j + 256])
+        g.remote_dma_fused([RemoteDMATransfer(dst_ids=ids, dma_engine_mask=topo.mask(core, T.cores[others[0]]), remote_sem=T.sem["fl%d" % r],
+                                              srcs=[T["FS%d" % r][:, :]], dsts=dsts)], local_sem=T.sem.ls)
+        sent += len(topo.engines(core, T.cores[others[0]]))
+        mark("rem", ("fl%d" % r, sum(len(topo.engines(T.cores[q], core)) for q in others)), [], [B("FR%d" % r)])
+        for j in range(3):
+            mm(B("pcut", 0, 256), B("IDB"), B("FR%d" % r, 256 * j, 256 * j + 256), False, j == 2)
+        ks, sk = ("FI", "AA")
+        if r > 0:
+            ks, sk = ("KS", "SK")
+            tt(B("pcnt", 272, 512), B("pcnt", 16, 256), B("CL", 16, 256), OP.min)
+            tt(B("SK", 16, 256), B("pcnt", 272, 512), B("AA", 16, 256), OP.max)
+            tree(B("KS", 0, 16), "SK", OP.max)
+        gat(B("OH"), B(ks, 0, 16), B("REP"), B(sk), OP.is_equal)
+        tt(B("PR", 16, 256), B("OH", 16, 256), B("pcr", 0, 240), OP.mult)
+        tree(B("TF"), "PR", OP.add)
+        cp(B("TL", 0, 32, 2), B("TF"))
+        cp(B("TL", 1, 32, 2), B("TF"))
+        act(B("X2"), B(xr, 0, 256), AF.Identity, scale=2.0, bias=255.75)
+        swap_in(B("PUW"), B("TL"))
+        t0 = "T0%d" % (r + 1)
+        tt(B(t0), B("pcut", 0, 256), B("T0%d" % r), OP.max)
+        dma("y", "dc%d" % r, T.TX[0:128:16, 0:4096], T[t0][:, :], [B(t0)], [B("TX")])
+        swap_out("CF")
+        cp(B("CU"), B("CF"))
+        high(B("CF"), B("TCH"))
+        minus257(B("TCH"))
+        distances("CU", xr, "CKE", "TCH", 0, [[(3, 4)], [(4, 8)], [(8, 12)], [(12, 14), (14, 16)]], lambda: None, True)
+        ts(B("TH"), B(ks, 0, 16), 0xFFF000, OP.bitwise_and)
+        tt(B("CB"), B("CF"), B("pcr", 256, 512), OP.add)
+        for q in range(4):
+            if q == 2:
+                tt(B("QR"), B("OH"), B("pcr", 0, 256), OP.mult)
+                tree(B("OLD"), "QR", OP.add)
+                if last:
+                    ts(B("YC"), B(t0), 1000.0, OP.is_ge)
+                    dma("y", "dyc", T.yc[:, :], T.YC[:, :], [B("YC")], [])
+            tt(B("BB", 64 * q, 64 * q + 64), B("pd%d" % q, 0, 64), B("CB", 64 * q, 64 * q + 64), OP.add)
+            if q == 0:
+                cp(B("RA", 0, 64), B("pd0", 0, 64))
+            else:
+                o = 64 * (q - 1)
+                tt(B("RA", o + 64, o + 128), B("RA", o, o + 64), B("pd%d" % q, 0, 64), OP.min)
+                tt(B("RB", o + 64, o + 128), B("BB" if q == 1 else "RB", o, o + 64), B("BB", 64 * q, 64 * q + 64), OP.min)
+        for run in ("RA", "RB"):
+            tt(B(run, 0, 32), B(run, 192, 224), B(run, 224, 256), OP.min)
+        for j, run in enumerate(("RA", "RB")):
+            tt(B("EI", 16 * j, 16 * j + 16), B(run, 0, 16), B(run, 16, 32), OP.min)
+        tt(B("LT"), B("EI", 0, 16), B("TH"), OP.is_lt)
+        ts(B("ET"), B("EI", 0, 16), 3840, OP.bitwise_and)
+        ts(B("EM"), B("EI"), 255, OP.bitwise_and)
+        tt(B("JJ"), B("ET"), B("VS"), OP.add)
+        ts(B("N1"), B("EM", 0, 16), 256.0, OP.mult)
+        tt(B("PO"), B("JJ"), B("LT"), OP.mult)
+        tt(B("BN"), B("N1"), B("EM", 16, 32), OP.add)
+        cp(B("POU"), B("PO"))
+        tt(B("DL"), B("BN"), B("OLD"), OP.subtract)
+        gat(B("XN"), B("D", 0, 4112), B("POU"), B("X2"), OP.add)
+        tt(B("DT"), B("DL"), B("LT"), OP.mult)
+        ts(B("XS%d" % r), B("XN"), 0.5, OP.mult, -128.0, OP.add)
+        gat(B("UP"), B("DT"), B("REP"), B("OH"), OP.mult)
+        ms = "MS%d" % r
+        tt(B(ms, 0, 256), B("UP"), B("pcr", 0, 256), OP.add)
+        if last:
+            gat(B("YX"), B("XS%d" % r), B("PERM"), None, None)
+            dma("y", "dyx", T.yx[:, :], T.YX[:, :], [B("YX")], [])
+            swap_in(B(ms, 0, 256), B("PERM2"))
+            swap_out("YP")
+            dma("y", "dyp", T.yp[:, :], T.YP[:, :], [B("YP")], [])
+            break
+        cp(B("PS%d" % r), B(ms, 0, 256))
+        need("g", [B("XS%d" % r), B("PS%d" % r)], [])
+        rid, pid = topo.addr(nxt)[:2]
+        eg = topo.engines(core, nxt)
+        half = len(eg) // 2
+        masks = [sum(1 << e for e in eg[:half]), sum(1 << e for e in eg[half:])]
+        dst = [DstId(rid=rid, pnc=pid)]
+        a1, a2 = "a1%d" % (r + 1), "a2%d" % (r + 1)
+        g.remote_dma_fused([
+            RemoteDMATransfer(dst_ids=dst, dma_engine_mask=masks[0], remote_sem=T.sem[a1], src=T["XS%d" % r][:, :],
+                              dst=T["XR%d" % (r + 1)][:, 0:256]),
+            RemoteDMATransfer(dst_ids=dst, dma_engine_mask=masks[1], remote_sem=T.sem[a1], src=T["PS%d" % r][:, :],
+                              dst=T["PU%d" % (r + 1)][:, :])], local_sem=T.sem.ls)
+        sent += len(eg)
+        n = len(topo.engines(prv, core))
+        mark("rem", (a1, n), [], [B("XR%d" % (r + 1), 0, 256), B("PU%d" % (r + 1))])
+        prep(ms)
+        need("g", [B(ms)], [])
+        g.remote_dma(T["M%d" % (r + 1)][:, :], T[ms][:, :], T.sem[a2], T.sem.ls, pid, rid, topo.mask(core, nxt))
+        sent += len(eg)
+        mark("rem", (a2, n), [], [B("M%d" % (r + 1))])
+    g.wait_ge(T.sem.ls, sent)
+    for e in "vstg":
+        g.wait_ge(T.sem["q" + e], cnt[e])
+    for s in ("dx0", "dp0", "dtx", "dpu", "dt0", "dyp", "dyx", "dyc") + tuple("dc%d" % r for r in range(R)):
+        g.wait_ge(T.sem[s], 16)

@@ -7,13 +7,13 @@ TOP = 8388608
 
 SCRATCH = {}
 SHAPES = {
-    "bfloat16": "TX 4096 X0 256 D 4112 AB 4096 OA 2048 OX 1024 OB 4096 LS 2048 IDM 128 IDN 128 IDB 128 IDT 128 GR 768 IOM 128 IM 128 IOB 256 "
-                "CKC 256 CKE 256 NEG 256 ONE 8 NE 128 TA 256 TCH 256 FB 32 XN 256 YX 256",
+    "bfloat16": "TX 4096 X0 256 D 4112 AB 4096 OA 2048 OX 1024 OB 4096 LS 2048 LX 2048 IDM 128 IDN 128 IDB 128 IDT 128 GR 768 IOM 128 IM 128 "
+                "IOB 256 CKC 256 CKE 256 NEG 256 ONE 8 NE 128 TCH 256 FB 32 XN 256 GX 256 YX 256",
     "int32": "PUW 4096 P0 256 I1 16 I2 16 I3 16 I5 16 PERMI 16 REPI 16 VS 16 GI 16 HI 16 FI 32 FM 32 KS 16 TH 16 EI 32 EM 32 ET 16 LT 16 "
-             "JJ 16 PO 16",
+             "JJ 16 PO 16 TO 16 TF 16 OLD 16",
     "uint16": "PERM 16 PERM2 32 REP 16 TL 32 CU 256 POU 16",
-    "float32": "MKI 512 MK 512 CL 256 COLS 16 COLP 16 COLH 16 SW 512 SWT 512 AA 256 BB 256 RA 256 RB 256 SK 256 KT 256 OH 256 PR 256 TF 16 "
-               "CF 256 CB 256 QR 256 OLD 16 X2 256 N1 16 BN 16 DL 16 DT 16 UP 256 YP 256 YC 256",
+    "float32": "MKI 512 MK 512 CL 256 COLS 16 COLP 16 COLH 16 SW 512 SWT 512 AA 256 RA 256 RB 256 SK 256 KT 256 OH 256 PR 128 "
+               "CF 256 CB 256 N1 16 BN 16 DL 16 DT 16 UP 256 YP 256 YC 256",
 }
 for _d, _l in SHAPES.items():
     _w = _l.split()
@@ -22,19 +22,20 @@ for _d, _l in SHAPES.items():
 for _n in ("pcr", "pcnt", "pchg", "pcut", "pd0", "pd1", "pd2", "pd3"):
     SCRATCH[_n] = ("psum", [128, 512], "float32")
 for _r in range(R):
+    SCRATCH["TR%d" % _r] = ("sbuf", [128, 256], "bfloat16")
+    SCRATCH["TS%d" % _r] = ("sbuf", [128, 256], "bfloat16")
     SCRATCH["XR%d" % _r] = ("sbuf", [128, 1024], "bfloat16")
     SCRATCH["PU%d" % _r] = ("sbuf", [128, 256], "uint16")
-    SCRATCH["M%d" % _r] = ("sbuf", [128, 768], "float32")
+    SCRATCH["M%d" % _r] = ("sbuf", [128, 1008], "float32")
     SCRATCH["XS%d" % _r] = ("sbuf", [128, 256], "bfloat16")
     SCRATCH["PS%d" % _r] = ("sbuf", [128, 256], "uint16")
-    SCRATCH["MS%d" % _r] = ("sbuf", [128, 768], "float32")
-    SCRATCH["FS%d" % _r] = ("sbuf", [128, 256], "bfloat16")
-    SCRATCH["FR%d" % _r] = ("sbuf", [128, 768], "bfloat16")
-for _r in range(R + 1):
-    SCRATCH["T0%d" % _r] = ("sbuf", [128, 256], "bfloat16")
+    SCRATCH["MS%d" % _r] = ("sbuf", [128, 1008], "float32")
+SCRATCH["FS"] = ("sbuf", [128, 256 * R], "bfloat16")
+SCRATCH["FR"] = ("sbuf", [128, 768 * R], "bfloat16")
+SCRATCH["T0"] = ("sbuf", [128, 256 * R + 256], "bfloat16")
 
 SEMAPHORES = ["qv", "qs", "qt", "qg", "ls", "dx0", "dp0", "dtx", "dpu", "dt0", "dyp", "dyx", "dyc"]
-SEMAPHORES += ["%s%d" % (a, r) for a in ("a1", "a2", "fl", "dc") for r in range(R)]
+SEMAPHORES += ["%s%d" % (a, r) for a in ("a1", "a2", "a3", "fl", "dc") for r in range(R)]
 
 
 def rank_program(g, core, T, topo):
@@ -63,7 +64,7 @@ def rank_program(g, core, T, topo):
             for name, lo, hi, _ in specs:
                 for plo, phi, pw, pe, tok in acc.get(name, ()):
                     if pe == e:
-                        hit = e != "t" and pw and not w and lo < phi and plo < hi
+                        hit = e != "t" and pw != w and lo < phi and plo < hi
                     elif psum(name):
                         hit = True
                     else:
@@ -122,6 +123,9 @@ def rank_program(g, core, T, topo):
         x = bias[3] if col else bias
         op("s", [a, bias] if col else [a], [out], lambda: g.scalar.activation(out[3], a[3], f, bias=x, scale=scale))
 
+    def sgat(out, win, lst):
+        op("s", [win, lst], [out], lambda: g.scalar.activation(out[3], win[3].indirect(lst[3]), AF.Copy))
+
     def mm(out, lhsT, rhs, start, stop):
         op("t", [lhsT, rhs], [out], lambda: g.tensor.matmul(out[3], lhsT[3], rhs[3], start, stop))
 
@@ -132,8 +136,8 @@ def rank_program(g, core, T, topo):
         else:
             op("g", [], [out], lambda: g.iota(out[3], pattern, base, cm, allow_small_or_imprecise_dtypes=True))
 
-    def tree(out, src, o):
-        tt(B("KT", 0, 128), B(src, 0, 128), B(src, 128, 256), o)
+    def tree(out, a, b, o):
+        tt(B("KT", 0, 128), a, b, o)
         tt(B("KT", 128, 192), B("KT", 0, 64), B("KT", 64, 128), o)
         tt(B("KT", 192, 224), B("KT", 128, 160), B("KT", 160, 192), o)
         tt(out, B("KT", 192, 208), B("KT", 208, 224), o)
@@ -152,32 +156,36 @@ def rank_program(g, core, T, topo):
     def minus257(ta):
         act(B("pcr", 256, 512), ta, AF.Identity, scale=-257.0, bias=257.0 * 160.0)
 
-    def prep(m):
+    def prep(m, ta):
         tt(B("NE"), B(m, 0, 256, 2), B(m, 1, 256, 2), OP.not_equal)
-        high(B(m, 0, 256), B("TA"))
-        minus257(B("TA"))
+        high(B(m, 0, 256), B(ta))
+        minus257(B(ta))
+        act(B("pcr", 0, 240), B(m, 0, 240), AF.Copy, scale=4096.0)
         for k in range(16):
-            mm(B("pcnt", 8 * k, 128), B("IDT"), B("NE", 0, 128 - 8 * k), k == 0, False)
-        mm(B("pcnt", 120, 128), B("IDT"), B("ONE"), False, True)
+            mm(B("pcut", 8 * k, 128), B("IDT"), B("NE", 0, 128 - 8 * k), k == 0, False)
+        mm(B("pcut", 120, 128), B("IDT"), B("ONE"), False, True)
+
+    def prep2(m):
         tt(B(m, 512, 768), B(m, 0, 256), B("pcr", 256, 512), OP.add)
         for p in (0, 1):
-            tt(B(m, 256 + p, 512, 2), B("pcnt", 0, 128), B("CL", p, 256, 2), OP.min)
+            tt(B(m, 256 + p, 512, 2), B("pcut", 0, 128), B("CL", p, 256, 2), OP.min)
+        tt(B(m, 768, 1008), B("pcr", 0, 240), B(m, 16, 256), OP.add)
 
     def distances(lst, xr, ck, ta, raw, chunks, later, keep):
-        op("s", [B("TX"), B(lst, 16 * raw, 16 * raw + 48)], [B("GR")],
-           lambda: g.scalar.activation(T.GR[:, :], T.TX[:, :].indirect(B(lst, 16 * raw, 16 * raw + 48)[3]), AF.Copy))
+        sgat(B("GR"), B("TX"), B(lst, 16 * raw, 16 * raw + 48))
         two, one = B("pcnt", 0, 512), B("pchg", 0, 256)
         mm(two, B("IDM"), B("GR", 0, 512), True, False)
-        mm(two, B("IDN"), B(xr, 0, 512), False, True)
+        mm(B("pcnt", 0, 256), B("IDN"), B(xr, 0, 256), False, False)
+        mm(B("pcnt", 256, 512), B("IDN"), B(xr, 0, 256), False, True)
         mm(one, B("IDM"), B("GR", 512, 768), True, False)
         mm(one, B("IDN"), B(xr, 0, 256), False, True)
         wait = []
         for q, calls in enumerate(chunks):
             for ka, kb in calls:
                 gat(B("D", 16 + 256 * ka, 16 + 256 * kb), B("TX"), B(lst, 16 * ka, 16 * kb), B(xr, 0, 256 * (kb - ka)), OP.subtract)
-            for ka, kb in ([(calls[0][0], calls[-1][1])] if q < 3 else calls):
-                act(B("AB", 256 * ka, 256 * kb), B("D", 16 + 256 * ka, 16 + 256 * kb), AF.Abs)
             ka, kb = calls[0][0], calls[-1][1]
+            for ja, jb in ([(ka, kb)] if q < 3 else [(ka, kb - 1), (kb - 1, kb)]):
+                act(B("AB", 256 * ja, 256 * jb), B("D", 16 + 256 * ja, 16 + 256 * jb), AF.Abs)
             if q == 0:
                 act(B("AB", 256 * raw, 256 * raw + 512), two, AF.Abs)
                 act(B("AB", 256 * raw + 512, 256 * raw + 768), one, AF.Abs)
@@ -199,7 +207,7 @@ def rank_program(g, core, T, topo):
     dma("y", "dp0", T.P0[:, :], T.p0[:, :], [], [B("P0")])
     dma("y", "dx0", T.X0[:, :], T.x0[:, :], [], [B("X0")])
     dma("y", "dtx", T.TX[:, :], T.tx[:, :], [], [B("TX")])
-    dma("y", "dt0", T.T00[:, :], T.tx[0:128:16, :], [], [B("T00")])
+    dma("y", "dt0", T.T0[:, 0:256], T.tx[0:128:16, :], [], [B("T0", 0, 256)])
     g.sync.wait_ge(T.sem.dtx, 16)
     dma("y", "dpu", T.PUW[:, :], T.pu[:, :], [], [B("PUW")])
 
@@ -234,6 +242,9 @@ def rank_program(g, core, T, topo):
     tt(B("VS"), B("REPI"), B("I3"), OP.add)
     ts(B("IDM"), B("IOM"), B("COLP", 0, 1), OP.is_equal)
     ts(B("IDN"), B("IOM"), B("COLP", 0, 1), OP.is_equal, -1.0, OP.mult)
+    for s in range(16):
+        act(B("LX", 128 * s, 128 * s + 128), B("IOM"), AF.Abs, scale=-1.0, bias=B("COLS", s, s + 1))
+    act(B("LS"), B("LX"), AF.Relu, scale=-4096.0, bias=4096.0)
     swap_in(B("P0"), B("PERM2"))
     swap_out("M0")
     cp(B("PU0"), B("M0", 0, 256))
@@ -242,40 +253,54 @@ def rank_program(g, core, T, topo):
     ts(B("IDB"), B("IOM"), B("COLP", 0, 1), OP.is_equal, BIG, OP.mult)
     ts(B("IM"), B("IOM"), B("COLS", 0, 1), OP.subtract)
     fill(B("CL", 0, 16), 0.0)
-    for s in range(16):
-        ts(B("LS", 128 * s, 128 * s + 128), B("IOM"), B("COLS", s, s + 1), OP.is_equal, 4096.0, OP.mult)
-    prep("M0")
 
     others = [q for q in range(R) if q != rank]
     nxt, prv = T.cores[(rank + 1) % R], T.cores[(rank - 1) % R]
+    rows = [(1, 5), (5, 9), (9, 13), (13, 16)]
+    singles = [[(k, k + 1) for k in range(max(a, 4), b)] for a, b in rows]
     sent = 0
     for r in range(R):
         xr, pu, m, last = "XR%d" % r, "PU%d" % r, "M%d" % r, r == R - 1
+        told, tnew = B("T0", 256 * r, 256 * r + 256), B("T0", 256 * r + 256, 256 * r + 512)
+        fs = B("FS", 256 * r, 256 * r + 256)
 
         def chain_arrays():
-            if r > 0:
-                high(B(m, 0, 256), B("TA"))
-            act(B("pcr", 0, 256), B(m, 0, 256), AF.Copy)
+            if r == 0:
+                prep(m, "TR0")
 
+        distances(pu, xr, "CKC", "TR%d" % r, 1, singles, chain_arrays, False)
         act(B(xr, 256, 512), B(xr, 0, 256), AF.Copy)
-        distances(pu, xr, "CKC", "TA", 1, [[(4, 5)], [(5, 7), (7, 9)], [(9, 11), (11, 13)], [(13, 15), (15, 16)]], chain_arrays, False)
         act(B(xr, 512, 1024), B(xr, 0, 512), AF.Copy)
-        rows = [(1, 5), (5, 9), (9, 13), (13, 16)]
-        for q, (ka, kb) in enumerate(rows):
-            ka, kb = 16 * ka, 16 * kb
+        if r == 0:
+            prep2(m)
+        act(B("pcr", 0, 240), B(m, 768, 1008), AF.Copy)
+
+        def key_a(q):
+            ka, kb = 16 * rows[q][0], 16 * rows[q][1]
             tt(B("AA", ka, kb), B("pd%d" % q, 0, kb - ka), B(m, 256 + ka, 256 + kb), OP.min)
-            tt(B("BB", ka, kb), B("AA", ka, kb), B(m, 512 + ka, 512 + kb), OP.add)
-            for src, run in (("AA", "RA"), ("BB", "RB")):
-                if q == 1:
-                    tt(B(run, 0, 64), B(src, 16, 80), B(src, 80, 144), OP.max)
-                elif q == 2:
-                    tt(B(run, 64, 128), B(run, 0, 64), B(src, 144, 208), OP.max)
-                elif q == 3:
-                    tt(B(run, 64, 112), B(run, 64, 112), B(src, 208, 256), OP.max)
+
+        def key_b(q):
+            ka, kb = 16 * rows[q][0], 16 * rows[q][1]
+            tt(B("RB", 0, 64) if q == 0 else B("pcut", 64 * q, 64 * q + kb - ka), B("AA", ka, kb), B(m, 512 + ka, 512 + kb), OP.add)
+
+        key_a(0)
+        key_a(1)
+        key_b(0)
+        tt(B("pcut", 256, 320), B("AA", 16, 80), B("AA", 80, 144), OP.max)
+        key_a(2)
+        key_b(1)
+        tt(B("RA", 64, 128), B("pcut", 256, 320), B("AA", 144, 208), OP.max)
+        tt(B("RB", 128, 192), B("RB", 0, 64), B("pcut", 64, 128), OP.max)
+        key_b(2)
+        key_a(3)
+        tt(B("RB", 64, 128), B("RB", 128, 192), B("pcut", 128, 192), OP.max)
+        key_b(3)
+        tt(B("RA", 64, 112), B("RA", 64, 112), B("AA", 208, 256), OP.max)
+        tt(B("RB", 64, 112), B("RB", 64, 112), B("pcut", 192, 240), OP.max)
         for run in ("RA", "RB"):
-            tt(B(run, 128, 160), B(run, 64, 96), B(run, 96, 128), OP.max)
+            tt(B(run, 192, 224), B(run, 64, 96), B(run, 96, 128), OP.max)
         for j, run in enumerate(("RA", "RB")):
-            tt(B("FI", 16 * j, 16 * j + 16), B(run, 128, 144), B(run, 144, 160), OP.max)
+            tt(B("FI", 16 * j, 16 * j + 16), B(run, 192, 208), B(run, 208, 224), OP.max)
         ts(B("FM"), B("FI"), 255, OP.bitwise_and)
         cp(B("FB"), B("FM"))
         for c in range(16):
@@ -289,63 +314,65 @@ def rank_program(g, core, T, topo):
             ts(B("OB", 256 * c, 256 * c + 256), B("IOB"), B("FB", 16 + c, 17 + c), OP.is_equal)
         for c in range(16):
             mm(B("pchg", 0, 256), B("OA", 128 * c, 128 * c + 128), B("OB", 256 * c, 256 * c + 256), c == 0, c == 15)
-        mm(B("pcut", 0, 256), B("IDM"), B("T0%d" % r), True, False)
+        mm(B("pcut", 0, 256), B("IDM"), told, True, False)
         mm(B("pcut", 0, 256), B("IDB"), B("NEG"), False, False)
         if r > 0:
             for q, (ka, kb) in enumerate(rows):
                 act(B("pcnt", 16 * ka, 16 * kb), B("pd%d" % q, 0, 16 * (kb - ka)), AF.Relu, bias=-16777216.0)
-        act(B("FS%d" % r), B("pchg", 0, 256), AF.Sign)
-        mm(B("pcut", 0, 256), B("IDB"), B("FS%d" % r), False, False)
-        need("g", [B("FS%d" % r)], [])
+        act(fs, B("pchg", 0, 256), AF.Sign)
+        mm(B("pcut", 0, 256), B("IDB"), fs, False, False)
+        need("g", [fs], [])
         dsts, ids = [], []
         for q in others:
-            j = (rank - q - 1) % R
+            j = 3 * r + (rank - q - 1) % R
             rid, pid = topo.addr(T.cores[q])[:2]
             ids.append(DstId(rid=rid, pnc=pid))
-            dsts.append(T["FR%d" % r][:, 256 * j:256 * j + 256])
+            dsts.append(T.FR[:, 256 * j:256 * j + 256])
         g.remote_dma_fused([RemoteDMATransfer(dst_ids=ids, dma_engine_mask=topo.mask(core, T.cores[others[0]]), remote_sem=T.sem["fl%d" % r],
-                                              srcs=[T["FS%d" % r][:, :]], dsts=dsts)], local_sem=T.sem.ls)
+                                              srcs=[fs[3]], dsts=dsts)], local_sem=T.sem.ls)
         sent += len(topo.engines(core, T.cores[others[0]]))
-        mark("rem", ("fl%d" % r, sum(len(topo.engines(T.cores[q], core)) for q in others)), [], [B("FR%d" % r)])
-        for j in range(3):
-            mm(B("pcut", 0, 256), B("IDB"), B("FR%d" % r, 256 * j, 256 * j + 256), False, j == 2)
+        mark("rem", ("fl%d" % r, sum(len(topo.engines(T.cores[q], core)) for q in others)), [], [B("FR", 768 * r, 768 * r + 768)])
+        for j in range(3 * r, 3 * r + 3):
+            mm(B("pcut", 0, 256), B("IDB"), B("FR", 256 * j, 256 * j + 256), False, j == 3 * r + 2)
         ks, sk = ("FI", "AA")
         if r > 0:
             ks, sk = ("KS", "SK")
             tt(B("pcnt", 272, 512), B("pcnt", 16, 256), B("CL", 16, 256), OP.min)
             tt(B("SK", 16, 256), B("pcnt", 272, 512), B("AA", 16, 256), OP.max)
-            tree(B("KS", 0, 16), "SK", OP.max)
+            tree(B("KS", 0, 16), B("SK", 0, 128), B("SK", 128, 256), OP.max)
         gat(B("OH"), B(ks, 0, 16), B("REP"), B(sk), OP.is_equal)
-        tt(B("PR", 16, 256), B("OH", 16, 256), B("pcr", 0, 240), OP.mult)
-        tree(B("TF"), "PR", OP.add)
+        tt(B("PR", 16, 128), B("OH", 16, 128), B("pcr", 0, 112), OP.mult)
+        tt(B("pchg", 0, 128), B("OH", 128, 256), B("pcr", 112, 240), OP.mult)
+        tree(B("TO"), B("PR"), B("pchg", 0, 128), OP.add)
+        ts(B("TF"), B("TO"), 12, OP.logical_shift_right)
         cp(B("TL", 0, 32, 2), B("TF"))
         cp(B("TL", 1, 32, 2), B("TF"))
-        act(B("X2"), B(xr, 0, 256), AF.Identity, scale=2.0, bias=255.75)
         swap_in(B("PUW"), B("TL"))
-        t0 = "T0%d" % (r + 1)
-        tt(B(t0), B("pcut", 0, 256), B("T0%d" % r), OP.max)
-        dma("y", "dc%d" % r, T.TX[0:128:16, 0:4096], T[t0][:, :], [B(t0)], [B("TX")])
+        tt(tnew, B("pcut", 0, 256), told, OP.max)
+        dma("y", "dc%d" % r, T.TX[0:128:16, 0:4096], tnew[3], [tnew], [B("TX")])
         swap_out("CF")
         cp(B("CU"), B("CF"))
         high(B("CF"), B("TCH"))
         minus257(B("TCH"))
-        distances("CU", xr, "CKE", "TCH", 0, [[(3, 4)], [(4, 8)], [(8, 12)], [(12, 14), (14, 16)]], lambda: None, True)
-        ts(B("TH"), B(ks, 0, 16), 0xFFF000, OP.bitwise_and)
+        if last:
+            ts(B("YC"), tnew, 1000.0, OP.is_ge)
+            dma("y", "dyc", T.yc[:, :], T.YC[:, :], [B("YC")], [])
+        distances("CU", xr, "CKE", "TCH", 0, [[(3, 4)], [(4, 8)], [(8, 12)], [(12, 15), (15, 16)]], lambda: None, True)
         tt(B("CB"), B("CF"), B("pcr", 256, 512), OP.add)
+        ts(B("TH"), B(ks, 0, 16), 0xFFF000, OP.bitwise_and)
+        ts(B("OLD"), B("TO"), 4095, OP.bitwise_and)
+        act(B("pcr", 0, 256), B(m, 0, 256), AF.Copy)
+        mm(B("pcnt", 0, 256), B("IDM"), B(xr, 0, 256), True, False)
+        mm(B("pcnt", 0, 256), B("IDM"), B(xr, 0, 256), False, False)
         for q in range(4):
-            if q == 2:
-                tt(B("QR"), B("OH"), B("pcr", 0, 256), OP.mult)
-                tree(B("OLD"), "QR", OP.add)
-                if last:
-                    ts(B("YC"), B(t0), 1000.0, OP.is_ge)
-                    dma("y", "dyc", T.yc[:, :], T.YC[:, :], [B("YC")], [])
-            tt(B("BB", 64 * q, 64 * q + 64), B("pd%d" % q, 0, 64), B("CB", 64 * q, 64 * q + 64), OP.add)
+            low = B("RB", 0, 64) if q == 0 else B("pcut", 64 * q, 64 * q + 64)
+            tt(low, B("pd%d" % q, 0, 64), B("CB", 64 * q, 64 * q + 64), OP.add)
             if q == 0:
                 cp(B("RA", 0, 64), B("pd0", 0, 64))
             else:
                 o = 64 * (q - 1)
                 tt(B("RA", o + 64, o + 128), B("RA", o, o + 64), B("pd%d" % q, 0, 64), OP.min)
-                tt(B("RB", o + 64, o + 128), B("BB" if q == 1 else "RB", o, o + 64), B("BB", 64 * q, 64 * q + 64), OP.min)
+                tt(B("RB", o + 64, o + 128), B("RB", o, o + 64), low, OP.min)
         for run in ("RA", "RB"):
             tt(B(run, 0, 32), B(run, 192, 224), B(run, 224, 256), OP.min)
         for j, run in enumerate(("RA", "RB")):
@@ -359,14 +386,16 @@ def rank_program(g, core, T, topo):
         tt(B("BN"), B("N1"), B("EM", 16, 32), OP.add)
         cp(B("POU"), B("PO"))
         tt(B("DL"), B("BN"), B("OLD"), OP.subtract)
-        gat(B("XN"), B("D", 0, 4112), B("POU"), B("X2"), OP.add)
+        sgat(B("GX"), B("D", 0, 4112), B("POU"))
+        mm(B("pcnt", 0, 256), B("IDM"), B("GX"), False, True)
+        act(B("XN"), B("pcnt", 0, 256), AF.Identity, bias=255.75)
         tt(B("DT"), B("DL"), B("LT"), OP.mult)
-        ts(B("XS%d" % r), B("XN"), 0.5, OP.mult, -128.0, OP.add)
+        act(B("XS%d" % r), B("XN"), AF.Identity, scale=0.5, bias=-128.0)
         gat(B("UP"), B("DT"), B("REP"), B("OH"), OP.mult)
         ms = "MS%d" % r
         tt(B(ms, 0, 256), B("UP"), B("pcr", 0, 256), OP.add)
         if last:
-            gat(B("YX"), B("XS%d" % r), B("PERM"), None, None)
+            sgat(B("YX"), B("XS%d" % r), B("PERM"))
             dma("y", "dyx", T.yx[:, :], T.YX[:, :], [B("YX")], [])
             swap_in(B(ms, 0, 256), B("PERM2"))
             swap_out("YP")
@@ -379,7 +408,7 @@ def rank_program(g, core, T, topo):
         half = len(eg) // 2
         masks = [sum(1 << e for e in eg[:half]), sum(1 << e for e in eg[half:])]
         dst = [DstId(rid=rid, pnc=pid)]
-        a1, a2 = "a1%d" % (r + 1), "a2%d" % (r + 1)
+        a1, a2, a3 = "a1%d" % (r + 1), "a2%d" % (r + 1), "a3%d" % (r + 1)
         g.remote_dma_fused([
             RemoteDMATransfer(dst_ids=dst, dma_engine_mask=masks[0], remote_sem=T.sem[a1], src=T["XS%d" % r][:, :],
                               dst=T["XR%d" % (r + 1)][:, 0:256]),
@@ -388,7 +417,13 @@ def rank_program(g, core, T, topo):
         sent += len(eg)
         n = len(topo.engines(prv, core))
         mark("rem", (a1, n), [], [B("XR%d" % (r + 1), 0, 256), B("PU%d" % (r + 1))])
-        prep(ms)
+        ta = "TS%d" % r
+        prep(ms, ta)
+        need("g", [B(ta)], [])
+        g.remote_dma(T["TR%d" % (r + 1)][:, :], T[ta][:, :], T.sem[a3], T.sem.ls, pid, rid, topo.mask(core, nxt))
+        sent += len(eg)
+        mark("rem", (a3, n), [], [B("TR%d" % (r + 1))])
+        prep2(ms)
         need("g", [B(ms)], [])
         g.remote_dma(T["M%d" % (r + 1)][:, :], T[ms][:, :], T.sem[a2], T.sem.ls, pid, rid, topo.mask(core, nxt))
         sent += len(eg)

from concourse.bass import DstId, RemoteDMATransfer
from concourse.mybir import AluOpType, ActivationFunctionType

R = 4
BIG = 16384.0
TOP = 8388608

SCRATCH = {}
SHAPES = {
    "bfloat16": "TX 4096 X0 256 D 4112 AB 4096 OA 2048 OX 1024 OB 4096 LS 2048 LX 2048 IDM 128 IDN 128 IDB 128 IDT 128 GR 768 IOM 128 IM 128 "
                "IOB 256 CKC 256 CKE 256 NEG 256 ONE 8 NE 128 TCH 256 FB 32 XN 256 GX 256 YX 256",
    "int32": "PUW 4096 P0 256 I1 16 I2 16 I3 16 I5 16 PERMI 16 REPI 16 VS 16 GI 16 HI 16 FI 32 FM 32 KS 16 TH 16 EI 32 EM 32 ET 16 LT 16 "
             "JJ 16 PO 16 TO 16 TF 16 OLD 16",
    "uint16": "PERM 16 PERM2 32 REP 16 TL 32 CU 256 POU 16",
    "float32": "MKI 512 MK 512 CL 256 COLS 16 COLP 16 COLH 16 SW 512 SWT 512 AA 256 RA 256 RB 256 SK 256 KT 256 OH 256 PR 128 "
               "CF 256 CB 256 N1 16 BN 16 DL 16 DT 16 UP 256 YP 256 YC 256",
}
for _d, _l in SHAPES.items():
    _w = _l.split()
    for _n, _c in zip(_w[::2], _w[1::2]):
        SCRATCH[_n] = ("sbuf", [128, int(_c)], _d)
for _n in ("pcr", "pcnt", "pchg", "pcut", "pd0", "pd1", "pd2", "pd3"):
    SCRATCH[_n] = ("psum", [128, 512], "float32")
for _r in range(R):
    SCRATCH["TR%d" % _r] = ("sbuf", [128, 256], "bfloat16")
    SCRATCH["TS%d" % _r] = ("sbuf", [128, 256], "bfloat16")
    SCRATCH["XR%d" % _r] = ("sbuf", [128, 1024], "bfloat16")
    SCRATCH["PU%d" % _r] = ("sbuf", [128, 256], "uint16")
    SCRATCH["M%d" % _r] = ("sbuf", [128, 1008], "float32")
    SCRATCH["XS%d" % _r] = ("sbuf", [128, 256], "bfloat16")
    SCRATCH["PS%d" % _r] = ("sbuf", [128, 256], "uint16")
    SCRATCH["MS%d" % _r] = ("sbuf", [128, 1008], "float32")
SCRATCH["FS"] = ("sbuf", [128, 256 * R], "bfloat16")
SCRATCH["FR"] = ("sbuf", [128, 768 * R], "bfloat16")
SCRATCH["T0"] = ("sbuf", [128, 256 * R + 256], "bfloat16")

SEMAPHORES = ["qv", "qs", "qt", "qg", "ls", "dx0", "dp0", "dtx", "dpu", "dt0", "dyp", "dyx", "dyc"]
SEMAPHORES += ["%s%d" % (a, r) for a in ("a1", "a2", "a3", "fl", "dc") for r in range(R)]


def rank_program(g, core, T, topo):
    rank = T.rank_of(core)
    if rank is None:
        return
    OP = AluOpType
    AF = ActivationFunctionType
    eng = {"v": g.vector, "s": g.scalar, "t": g.tensor, "g": g, "y": g.sync}
    cnt = {"v": 0, "s": 0, "t": 0, "g": 0}
    known = {e: {} for e in eng}
    acc = {}

    def B(name, lo=0, hi=None, step=1):
        if hi is None:
            hi = SCRATCH[name][1][1]
        ap = T[name][:, lo:hi] if step == 1 else T[name][:, lo:hi:step]
        return (name, lo, hi, ap)

    def psum(name):
        return SCRATCH[name][0] == "psum"

    def need(e, reads, writes):
        deps = {}
        for w, specs in ((False, reads), (True, writes)):
            for name, lo, hi, _ in specs:
                for plo, phi, pw, pe, tok in acc.get(name, ()):
                    if pe == e:
                        hit = e != "t" and pw != w and lo < phi and plo < hi
                    elif psum(name):
                        hit = True
                    else:
                        hit = (pw or w) and lo < phi and plo < hi
                    if hit and deps.get(tok[0], 0) < tok[1]:
                        deps[tok[0]] = tok[1]
        for sem in sorted(deps):
            if known[e].get(sem, 0) < deps[sem]:
                eng[e].wait_ge(T.sem[sem], deps[sem])
                known[e][sem] = deps[sem]

    def mark(pe, tok, reads, writes):
        for name, lo, hi, _ in writes:
            old = [a for a in acc.get(name, ()) if not (lo <= a[0] and a[1] <= hi)]
            acc[name] = old + [(lo, hi, True, pe, tok)]
        for name, lo, hi, _ in reads:
            old = [a for a in acc.get(name, ()) if not (a[3] == pe and not a[2] and lo <= a[0] and a[1] <= hi)]
            acc[name] = old + [(lo, hi, False, pe, tok)]

    def op(e, reads, writes, fn):
        need(e, reads, writes)
        fn().then_inc(T.sem["q" + e], 1)
        cnt[e] += 1
        mark(e, ("q" + e, cnt[e]), reads, writes)

    def dma(e, sem, out, in_, reads, writes):
        need(e, reads, writes)
        eng[e].dma_start(out, in_).then_inc(T.sem[sem], 16)
        mark("d" + sem, (sem, 16), reads, writes)

    def tt(out, a, b, o):
        op("v", [a, b], [out], lambda: g.vector.tensor_tensor(out[3], a[3], b[3], o))

    def ts(out, a, s1, o1, s2=None, o2=None):
        reads = [a] + [s for s in (s1,) if isinstance(s, tuple)]
        x = s1[3] if isinstance(s1, tuple) else s1
        if o2 is None:
            op("v", reads, [out], lambda: g.vector.tensor_scalar(out[3], a[3], x, None, o1))
        else:
            op("v", reads, [out], lambda: g.vector.tensor_scalar(out[3], a[3], x, s2, o1, o2))

    def cp(out, a):
        op("v", [a], [out], lambda: g.vector.tensor_copy(out[3], a[3]))

    def gat(out, win, lst, b, o):
        if b is None:
            op("v", [win, lst], [out], lambda: g.vector.tensor_copy(out[3], win[3].indirect(lst[3])))
        else:
            op("v", [win, lst, b], [out], lambda: g.vector.tensor_tensor(out[3], win[3].indirect(lst[3]), b[3], o))

    def fill(out, value):
        op("v", [], [out], lambda: g.vector.memset(out[3], value))

    def act(out, a, f, scale=1.0, bias=0.0):
        col = isinstance(bias, tuple)
        x = bias[3] if col else bias
        op("s", [a, bias] if col else [a], [out], lambda: g.scalar.activation(out[3], a[3], f, bias=x, scale=scale))

    def sgat(out, win, lst):
        op("s", [win, lst], [out], lambda: g.scalar.activation(out[3], win[3].indirect(lst[3]), AF.Copy))

    def mm(out, lhsT, rhs, start, stop):
        op("t", [lhsT, rhs], [out], lambda: g.tensor.matmul(out[3], lhsT[3], rhs[3], start, stop))

    def iota(name, pattern, base, cm):
        out = B(name)
        if SCRATCH[name][2] == "int32":
            op("g", [], [out], lambda: g.iota(out[3], pattern, base, cm))
        else:
            op("g", [], [out], lambda: g.iota(out[3], pattern, base, cm, allow_small_or_imprecise_dtypes=True))

    def tree(out, a, b, o):
        tt(B("KT", 0, 128), a, b, o)
        tt(B("KT", 128, 192), B("KT", 0, 64), B("KT", 64, 128), o)
        tt(B("KT", 192, 224), B("KT", 128, 160), B("KT", 160, 192), o)
        tt(out, B("KT", 192, 208), B("KT", 208, 224), o)

    def swap_in(win, lst):
        gat(B("SW"), win, lst, B("MK"), OP.mult)
        op("v", [B("SW")], [B("SWT")], lambda: g.vector.transpose(T.SWT[:, :], T.SW[:, :]))

    def swap_out(name):
        for t in range(16):
            tt(B(name, 16 * t, 16 * t + 16), B("SWT", t, 512, 32), B("SWT", 16 + t, 512, 32), OP.add)

    def high(src, ta):
        act(ta, src, AF.Identity, scale=1.0 / 256.0, bias=159.502)

    def minus257(ta):
        act(B("pcr", 256, 512), ta, AF.Identity, scale=-257.0, bias=257.0 * 160.0)

    def prep(m, ta):
        tt(B("NE"), B(m, 0, 256, 2), B(m, 1, 256, 2), OP.not_equal)
        high(B(m, 0, 256), B(ta))
        minus257(B(ta))
        act(B("pcr", 0, 240), B(m, 0, 240), AF.Copy, scale=4096.0)
        for k in range(16):
            mm(B("pcut", 8 * k, 128), B("IDT"), B("NE", 0, 128 - 8 * k), k == 0, False)
        mm(B("pcut", 120, 128), B("IDT"), B("ONE"), False, True)

    def prep2(m):
        tt(B(m, 512, 768), B(m, 0, 256), B("pcr", 256, 512), OP.add)
        for p in (0, 1):
            tt(B(m, 256 + p, 512, 2), B("pcut", 0, 128), B("CL", p, 256, 2), OP.min)
        tt(B(m, 768, 1008), B("pcr", 0, 240), B(m, 16, 256), OP.add)

    def distances(lst, xr, ck, ta, raw, chunks, later, keep):
        sgat(B("GR"), B("TX"), B(lst, 16 * raw, 16 * raw + 48))
        two, one = B("pcnt", 0, 512), B("pchg", 0, 256)
        mm(two, B("IDM"), B("GR", 0, 512), True, False)
        mm(B("pcnt", 0, 256), B("IDN"), B(xr, 0, 256), False, False)
        mm(B("pcnt", 256, 512), B("IDN"), B(xr, 0, 256), False, True)
        mm(one, B("IDM"), B("GR", 512, 768), True, False)
        mm(one, B("IDN"), B(xr, 0, 256), False, True)
        wait = []
        for q, calls in enumerate(chunks):
            for ka, kb in calls:
                gat(B("D", 16 + 256 * ka, 16 + 256 * kb), B("TX"), B(lst, 16 * ka, 16 * kb), B(xr, 0, 256 * (kb - ka)), OP.subtract)
            ka, kb = calls[0][0], calls[-1][1]
            for ja, jb in ([(ka, kb)] if q < 3 else [(ka, kb - 1), (kb - 1, kb)]):
                act(B("AB", 256 * ja, 256 * jb), B("D", 16 + 256 * ja, 16 + 256 * jb), AF.Abs)
            if q == 0:
                act(B("AB", 256 * raw, 256 * raw + 512), two, AF.Abs)
                act(B("AB", 256 * raw + 512, 256 * raw + 768), one, AF.Abs)
                ka = raw
            if q == 1:
                later()
            ps = B("pd%d" % q, 0, 16 * (kb - ka))
            mm(ps, B("IDM"), B(ck, 16 * ka, 16 * kb), True, False)
            for s in range(16):
                mm(ps, B("LS", 128 * s, 128 * s + 128), B("AB", 256 * ka + s, 256 * kb, 16), False, False)
            wait.append((ps, B(ta, 16 * ka, 16 * kb)))
            while q > 0 and wait:
                ps, dig = wait.pop(0)
                mm(ps, B("IDM"), dig, False, True)
        if keep:
            act(B("D", 16 + 256 * raw, 16 + 256 * raw + 512), two, AF.Copy)
            act(B("D", 16 + 256 * raw + 512, 16 + 256 * raw + 768), one, AF.Copy)

    dma("y", "dp0", T.P0[:, :], T.p0[:, :], [], [B("P0")])
    dma("y", "dx0", T.X0[:, :], T.x0[:, :], [], [B("X0")])
    dma("y", "dtx", T.TX[:, :], T.tx[:, :], [], [B("TX")])
    dma("y", "dt0", T.T0[:, 0:256], T.tx[0:128:16, :], [], [B("T0", 0, 256)])
    g.sync.wait_ge(T.sem.dtx, 16)
    dma("y", "dpu", T.PUW[:, :], T.pu[:, :], [], [B("PUW")])

    iota("I1", [[1, 16]], 0, 16)
    iota("I2", [[0, 16]], 0, 1)
    iota("MKI", [[0, 16], [1, 2], [0, 16]], 0, 0)
    iota("IOM", [[1, 128]], 0, 0)
    iota("I5", [[1, 16]], 0, 0)
    iota("I3", [[16, 16]], 16, 0)
    iota("CL", [[-256, 16], [0, 16]], TOP + 4096 + 255, 0)
    iota("CKC", [[-256, 16], [0, 16]], 4096 - 160, 0)
    iota("IOB", [[1, 256]], 0, 0)
    iota("CKE", [[256, 16], [0, 16]], -160, 0)
    fill(B("ONE"), 1.0)
    fill(B("NEG"), -1.0)
    fill(B("D", 0, 16), 0.0)
    fill(B("AA", 0, 16), 0.0)
    fill(B("PR", 0, 16), 0.0)
    fill(B("SK", 0, 16), 0.0)
    ts(B("PERMI"), B("I1"), 255, OP.bitwise_and)
    ts(B("HI"), B("I2"), 16, OP.bitwise_and, 4, OP.logical_shift_right)
    ts(B("REPI"), B("I2"), 15, OP.bitwise_and)
    ts(B("GI"), B("I2"), 112, OP.bitwise_and)
    cp(B("PERM"), B("PERMI"))
    cp(B("PERM2", 0, 32, 2), B("PERMI"))
    cp(B("PERM2", 1, 32, 2), B("PERMI"))
    cp(B("COLH"), B("HI"))
    cp(B("COLP"), B("I2"))
    cp(B("REP"), B("REPI"))
    ts(B("MK"), B("MKI"), B("COLH", 0, 1), OP.is_equal)
    tt(B("COLS"), B("GI"), B("I5"), OP.add)
    tt(B("VS"), B("REPI"), B("I3"), OP.add)
    ts(B("IDM"), B("IOM"), B("COLP", 0, 1), OP.is_equal)
    ts(B("IDN"), B("IOM"), B("COLP", 0, 1), OP.is_equal, -1.0, OP.mult)
    for s in range(16):
        act(B("LX", 128 * s, 128 * s + 128), B("IOM"), AF.Abs, scale=-1.0, bias=B("COLS", s, s + 1))
    act(B("LS"), B("LX"), AF.Relu, scale=-4096.0, bias=4096.0)
    swap_in(B("P0"), B("PERM2"))
    swap_out("M0")
    cp(B("PU0"), B("M0", 0, 256))
    gat(B("XR0", 0, 256), B("X0"), B("PERM"), None, None)
    ts(B("IDT"), B("IOM"), B("COLP", 0, 1), OP.is_equal, 16777216.0, OP.mult)
    ts(B("IDB"), B("IOM"), B("COLP", 0, 1), OP.is_equal, BIG, OP.mult)
    ts(B("IM"), B("IOM"), B("COLS", 0, 1), OP.subtract)
    fill(B("CL", 0, 16), 0.0)

    others = [q for q in range(R) if q != rank]
    nxt, prv = T.cores[(rank + 1) % R], T.cores[(rank - 1) % R]
    rows = [(1, 5), (5, 9), (9, 13), (13, 16)]
    singles = [[(k, k + 1) for k in range(max(a, 4), b)] for a, b in rows]
    sent = 0
    for r in range(R):
        xr, pu, m, last = "XR%d" % r, "PU%d" % r, "M%d" % r, r == R - 1
        told, tnew = B("T0", 256 * r, 256 * r + 256), B("T0", 256 * r + 256, 256 * r + 512)
        fs = B("FS", 256 * r, 256 * r + 256)

        def chain_arrays():
            if r == 0:
                prep(m, "TR0")

        distances(pu, xr, "CKC", "TR%d" % r, 1, singles, chain_arrays, False)
        act(B(xr, 256, 512), B(xr, 0, 256), AF.Copy)
        act(B(xr, 512, 1024), B(xr, 0, 512), AF.Copy)
        if r == 0:
            prep2(m)
        act(B("pcr", 0, 240), B(m, 768, 1008), AF.Copy)

        def key_a(q):
            ka, kb = 16 * rows[q][0], 16 * rows[q][1]
            tt(B("AA", ka, kb), B("pd%d" % q, 0, kb - ka), B(m, 256 + ka, 256 + kb), OP.min)

        def key_b(q):
            ka, kb = 16 * rows[q][0], 16 * rows[q][1]
            tt(B("RB", 0, 64) if q == 0 else B("pcut", 64 * q, 64 * q + kb - ka), B("AA", ka, kb), B(m, 512 + ka, 512 + kb), OP.add)

        key_a(0)
        key_a(1)
        key_b(0)
        tt(B("pcut", 256, 320), B("AA", 16, 80), B("AA", 80, 144), OP.max)
        key_a(2)
        key_b(1)
        tt(B("RA", 64, 128), B("pcut", 256, 320), B("AA", 144, 208), OP.max)
        tt(B("RB", 128, 192), B("RB", 0, 64), B("pcut", 64, 128), OP.max)
        key_b(2)
        key_a(3)
        tt(B("RB", 64, 128), B("RB", 128, 192), B("pcut", 128, 192), OP.max)
        key_b(3)
        tt(B("RA", 64, 112), B("RA", 64, 112), B("AA", 208, 256), OP.max)
        tt(B("RB", 64, 112), B("RB", 64, 112), B("pcut", 192, 240), OP.max)
        for run in ("RA", "RB"):
            tt(B(run, 192, 224), B(run, 64, 96), B(run, 96, 128), OP.max)
        for j, run in enumerate(("RA", "RB")):
            tt(B("FI", 16 * j, 16 * j + 16), B(run, 192, 208), B(run, 208, 224), OP.max)
        ts(B("FM"), B("FI"), 255, OP.bitwise_and)
        cp(B("FB"), B("FM"))
        for c in range(16):
            if c < 8:
                ts(B("OA", 128 * c, 128 * c + 128), B("IM"), B("FB", c, c + 1), OP.is_equal)
            else:
                j = c - 8
                act(B("OX", 128 * j, 128 * j + 128), B("IM"), AF.Abs, scale=-1.0, bias=B("FB", c, c + 1))
                if c % 4 == 3:
                    act(B("OA", 128 * c - 384, 128 * c + 128), B("OX", 128 * j - 384, 128 * j + 128), AF.Relu, scale=-1.0, bias=1.0)
            ts(B("OB", 256 * c, 256 * c + 256), B("IOB"), B("FB", 16 + c, 17 + c), OP.is_equal)
        for c in range(16):
            mm(B("pchg", 0, 256), B("OA", 128 * c, 128 * c + 128), B("OB", 256 * c, 256 * c + 256), c == 0, c == 15)
        mm(B("pcut", 0, 256), B("IDM"), told, True, False)
        mm(B("pcut", 0, 256), B("IDB"), B("NEG"), False, False)
        if r > 0:
            for q, (ka, kb) in enumerate(rows):
                act(B("pcnt", 16 * ka, 16 * kb), B("pd%d" % q, 0, 16 * (kb - ka)), AF.Relu, bias=-16777216.0)
        act(fs, B("pchg", 0, 256), AF.Sign)
        mm(B("pcut", 0, 256), B("IDB"), fs, False, False)
        need("g", [fs], [])
        dsts, ids = [], []
        for q in others:
            j = 3 * r + (rank - q - 1) % R
            rid, pid = topo.addr(T.cores[q])[:2]
            ids.append(DstId(rid=rid, pnc=pid))
            dsts.append(T.FR[:, 256 * j:256 * j + 256])
        g.remote_dma_fused([RemoteDMATransfer(dst_ids=ids, dma_engine_mask=topo.mask(core, T.cores[others[0]]), remote_sem=T.sem["fl%d" % r],
                                              srcs=[fs[3]], dsts=dsts)], local_sem=T.sem.ls)
        sent += len(topo.engines(core, T.cores[others[0]]))
        mark("rem", ("fl%d" % r, sum(len(topo.engines(T.cores[q], core)) for q in others)), [], [B("FR", 768 * r, 768 * r + 768)])
        for j in range(3 * r, 3 * r + 3):
            mm(B("pcut", 0, 256), B("IDB"), B("FR", 256 * j, 256 * j + 256), False, j == 3 * r + 2)
        ks, sk = ("FI", "AA")
        if r > 0:
            ks, sk = ("KS", "SK")
            tt(B("pcnt", 272, 512), B("pcnt", 16, 256), B("CL", 16, 256), OP.min)
            tt(B("SK", 16, 256), B("pcnt", 272, 512), B("AA", 16, 256), OP.max)
            tree(B("KS", 0, 16), B("SK", 0, 128), B("SK", 128, 256), OP.max)
        gat(B("OH"), B(ks, 0, 16), B("REP"), B(sk), OP.is_equal)
        tt(B("PR", 16, 128), B("OH", 16, 128), B("pcr", 0, 112), OP.mult)
        tt(B("pchg", 0, 128), B("OH", 128, 256), B("pcr", 112, 240), OP.mult)
        tree(B("TO"), B("PR"), B("pchg", 0, 128), OP.add)
        ts(B("TF"), B("TO"), 12, OP.logical_shift_right)
        cp(B("TL", 0, 32, 2), B("TF"))
        cp(B("TL", 1, 32, 2), B("TF"))
        swap_in(B("PUW"), B("TL"))
        tt(tnew, B("pcut", 0, 256), told, OP.max)
        dma("y", "dc%d" % r, T.TX[0:128:16, 0:4096], tnew[3], [tnew], [B("TX")])
        swap_out("CF")
        cp(B("CU"), B("CF"))
        high(B("CF"), B("TCH"))
        minus257(B("TCH"))
        if last:
            ts(B("YC"), tnew, 1000.0, OP.is_ge)
            dma("y", "dyc", T.yc[:, :], T.YC[:, :], [B("YC")], [])
        distances("CU", xr, "CKE", "TCH", 0, [[(3, 4)], [(4, 8)], [(8, 12)], [(12, 15), (15, 16)]], lambda: None, True)
        tt(B("CB"), B("CF"), B("pcr", 256, 512), OP.add)
        ts(B("TH"), B(ks, 0, 16), 0xFFF000, OP.bitwise_and)
        ts(B("OLD"), B("TO"), 4095, OP.bitwise_and)
        act(B("pcr", 0, 256), B(m, 0, 256), AF.Copy)
        mm(B("pcnt", 0, 256), B("IDM"), B(xr, 0, 256), True, False)
        mm(B("pcnt", 0, 256), B("IDM"), B(xr, 0, 256), False, False)
        for q in range(4):
            low = B("RB", 0, 64) if q == 0 else B("pcut", 64 * q, 64 * q + 64)
            tt(low, B("pd%d" % q, 0, 64), B("CB", 64 * q, 64 * q + 64), OP.add)
            if q == 0:
                cp(B("RA", 0, 64), B("pd0", 0, 64))
            else:
                o = 64 * (q - 1)
                tt(B("RA", o + 64, o + 128), B("RA", o, o + 64), B("pd%d" % q, 0, 64), OP.min)
                tt(B("RB", o + 64, o + 128), B("RB", o, o + 64), low, OP.min)
        for run in ("RA", "RB"):
            tt(B(run, 0, 32), B(run, 192, 224), B(run, 224, 256), OP.min)
        for j, run in enumerate(("RA", "RB")):
            tt(B("EI", 16 * j, 16 * j + 16), B(run, 0, 16), B(run, 16, 32), OP.min)
        tt(B("LT"), B("EI", 0, 16), B("TH"), OP.is_lt)
        ts(B("ET"), B("EI", 0, 16), 3840, OP.bitwise_and)
        ts(B("EM"), B("EI"), 255, OP.bitwise_and)
        tt(B("JJ"), B("ET"), B("VS"), OP.add)
        ts(B("N1"), B("EM", 0, 16), 256.0, OP.mult)
        tt(B("PO"), B("JJ"), B("LT"), OP.mult)
        tt(B("BN"), B("N1"), B("EM", 16, 32), OP.add)
        cp(B("POU"), B("PO"))
        tt(B("DL"), B("BN"), B("OLD"), OP.subtract)
        sgat(B("GX"), B("D", 0, 4112), B("POU"))
        mm(B("pcnt", 0, 256), B("IDM"), B("GX"), False, True)
        act(B("XN"), B("pcnt", 0, 256), AF.Identity, bias=255.75)
        tt(B("DT"), B("DL"), B("LT"), OP.mult)
        act(B("XS%d" % r), B("XN"), AF.Identity, scale=0.5, bias=-128.0)
        gat(B("UP"), B("DT"), B("REP"), B("OH"), OP.mult)
        ms = "MS%d" % r
        tt(B(ms, 0, 256), B("UP"), B("pcr", 0, 256), OP.add)
        if last:
            sgat(B("YX"), B("XS%d" % r), B("PERM"))
            dma("y", "dyx", T.yx[:, :], T.YX[:, :], [B("YX")], [])
            swap_in(B(ms, 0, 256), B("PERM2"))
            swap_out("YP")
            dma("y", "dyp", T.yp[:, :], T.YP[:, :], [B("YP")], [])
            break
        cp(B("PS%d" % r), B(ms, 0, 256))
        need("g", [B("XS%d" % r), B("PS%d" % r)], [])
        rid, pid = topo.addr(nxt)[:2]
        eg = topo.engines(core, nxt)
        half = len(eg) // 2
        masks = [sum(1 << e for e in eg[:half]), sum(1 << e for e in eg[half:])]
        dst = [DstId(rid=rid, pnc=pid)]
        a1, a2, a3 = "a1%d" % (r + 1), "a2%d" % (r + 1), "a3%d" % (r + 1)
        g.remote_dma_fused([
            RemoteDMATransfer(dst_ids=dst, dma_engine_mask=masks[0], remote_sem=T.sem[a1], src=T["XS%d" % r][:, :],
                              dst=T["XR%d" % (r + 1)][:, 0:256]),
            RemoteDMATransfer(dst_ids=dst, dma_engine_mask=masks[1], remote_sem=T.sem[a1], src=T["PS%d" % r][:, :],
                              dst=T["PU%d" % (r + 1)][:, :])], local_sem=T.sem.ls)
        sent += len(eg)
        n = len(topo.engines(prv, core))
        mark("rem", (a1, n), [], [B("XR%d" % (r + 1), 0, 256), B("PU%d" % (r + 1))])
        ta = "TS%d" % r
        prep(ms, ta)
        need("g", [B(ta)], [])
        g.remote_dma(T["TR%d" % (r + 1)][:, :], T[ta][:, :], T.sem[a3], T.sem.ls, pid, rid, topo.mask(core, nxt))
        sent += len(eg)
        mark("rem", (a3, n), [], [B("TR%d" % (r + 1))])
        prep2(ms)
        need("g", [B(ms)], [])
        g.remote_dma(T["M%d" % (r + 1)][:, :], T[ms][:, :], T.sem[a2], T.sem.ls, pid, rid, topo.mask(core, nxt))
        sent += len(eg)
        mark("rem", (a2, n), [], [B("M%d" % (r + 1))])
    g.wait_ge(T.sem.ls, sent)
    for e in "vstg":
        g.wait_ge(T.sem["q" + e], cnt[e])
    for s in ("dx0", "dp0", "dtx", "dpu", "dt0", "dyp", "dyx", "dyc") + tuple("dc%d" % r for r in range(R)):
        g.wait_ge(T.sem[s], 16)
